import numpy as np
import ml_dtypes


def mxq(x, axis, fmt="e4m3"):
    dtype, down = {"e4m3": (ml_dtypes.float8_e4m3fn, 7), "e5m2": (ml_dtypes.float8_e5m2, 14)}[fmt]
    v = np.moveaxis(np.asarray(x, np.float32).astype(ml_dtypes.bfloat16).astype(np.float64), axis, -1)
    blocks = v.reshape(v.shape[:-1] + (-1, 32))
    amax = np.abs(blocks).max(-1, keepdims=True)
    byte = np.maximum(np.where(amax > 0, np.frexp(amax)[1] - 1 + 127, 0) - down, 1)
    scale = np.exp2(byte - 127.0)
    codes = (blocks / scale).astype(np.float32).astype(dtype).astype(np.float64)
    return np.moveaxis((codes * scale).reshape(v.shape), -1, axis)


WIDE = False


def mx_kscale(k):
    if not WIDE:
        return np.ones(k)
    levels = np.array([10, -10, 5, -5, 0])
    if k % 512:
        return np.exp2(np.random.permutation(np.resize(levels, k // 32))).repeat(32)
    a = np.empty((k // 512, 16))
    for p in range(k // 512):
        a[p, :8] = np.random.permutation(np.resize(levels, 8))
        for g in range(8):
            far = levels[np.abs(levels - a[p, g]) >= 10]
            a[p, g + 8] = far[np.random.randint(len(far))]
    return np.exp2(a.ravel()).repeat(32)


def f64(x):
    return np.asarray(x).astype(np.float64)


def striped(idx):
    return np.tile(idx.reshape(-1, 16).T, (8, 1)).astype(np.uint16)


def unstriped(offs):
    return offs[:16].T.reshape(-1).astype(np.int64)


def pack_weight(w):
    k, n = w.shape
    w = f64(np.asarray(w, np.float32).astype(ml_dtypes.bfloat16)).reshape(k // 32, 32, n)
    amax = np.abs(w).max(1)
    byte = np.clip(np.where(amax > 0, np.frexp(amax)[1] - 1 + 127 - 7, 1), 1, 254)
    scaled = (w * np.exp2(127.0 - byte)[:, None, :]).reshape(k, n).astype(np.float32)
    words = np.ascontiguousarray(scaled.reshape(k // 512, 128, 4, n).transpose(0, 1, 3, 2)).astype(ml_dtypes.float8_e4m3fn).view(np.uint8)
    return words, np.ascontiguousarray(byte.astype(np.uint8).reshape(k // 512, 16, n))


def unpack_weight(words, scales):
    g, p, n, _ = words.shape
    vals = np.ascontiguousarray(words).view(ml_dtypes.float8_e4m3fn).astype(np.float64) * np.repeat(np.exp2(scales.astype(np.float64) - 127.0), 8, axis=1)[..., None]
    return vals.transpose(0, 1, 3, 2).reshape(g * 512, n)


def relu(v):
    return np.maximum(v, 0.0)


def sigmoid(v):
    return 1.0 / (1.0 + np.exp(-np.maximum(v, -700.0)))


K, T, S, D, N = 512, 4096, 1024, 4, 256
P = 2 ** 7


def setup_inputs():
    n = np.random.standard_normal
    s = mx_kscale(K)[:, None]
    packed_xT = pack_weight(n((K, T)) * s)
    return {
        "x_words": packed_xT[0],
        "x_scales": packed_xT[1],
        "w1": (n((K, N)) / np.sqrt(K) / s).astype(np.float32),
        "w2": (n((K, N)) / np.sqrt(K) / s).astype(np.float32),
        "w3": (n((K, N)) / np.sqrt(K) / s).astype(np.float32),
        "fmax": (np.tile(np.random.uniform(0.6, 1.8, S), (P, 1))).astype(np.float32),
        "arm": (np.tile(np.random.uniform(-1.0, 1.0, S), (P, 1))).astype(np.float32),
        "offs": striped(np.random.permutation(T)[:S]),
    }


def reference(x_words, x_scales, w1, w2, w3, fmax, arm, offs):
    xq = unpack_weight(x_words, x_scales)[:, unstriped(offs)]
    ya = mxq(f64(w3), 0, "e4m3").T @ xq
    actv = sigmoid(ya)
    yl = mxq(f64(w1), 0, "e4m3").T @ xq
    flen = np.exp(-0.8 * ((yl) ** 2))
    yv = mxq(f64(w2), 0, "e4m3").T @ xq
    vel = np.tanh(yv)
    fvel = (-1.0 * vel + 1.0) / (0.6 * vel + 1.3)
    frc = f64(fmax)[:1] * ((actv * flen) * fvel + 0.4 * (relu(np.exp(0.9 * yl) - 1.0)))
    mom = frc * f64(arm)[:1]
    return mom.reshape(len(mom), -1, D).sum(axis=2)

@@ -1,0 +1,223 @@
+import math
+from contextlib import ExitStack
+
+import concourse.mybir as mybir
+from concourse.masks import make_identity
+
+K, T, S, D, N = 512, 4096, 1024, 4, 256
+FLOPS = 3 * 2 * K * N * S
+BYTES = K * T + (K // 32) * T + 3 * K * N * 4 + 2 * S * 4 + 128 * (S // 16) * 2 + N * (S // D) * 4
+
+F32 = mybir.dt.float32
+BF16 = mybir.dt.bfloat16
+I32 = mybir.dt.int32
+U32 = mybir.dt.uint32
+U16 = mybir.dt.uint16
+U8 = mybir.dt.uint8
+FP8X4 = mybir.dt.float8_e4m3fn_x4
+ALU = mybir.AluOpType
+ACT = mybir.ActivationFunctionType
+
+P = 128
+PACK = 4
+HALVES = 2
+HALF = S // HALVES
+PAIRS = 2
+
+
+def tile_picked_yhillm_mom_p_kernel(
+    tc, x_words, x_scales, w1, w2, w3, fmax, arm, offs, out
+):
+    nc = tc.nc
+    with ExitStack() as ctx:
+        keep = ctx.enter_context(tc.tile_pool(name="keep", bufs=1))
+        psum = ctx.enter_context(tc.psum_pool(name="psum", bufs=1))
+
+        offsets = keep.tile([P, S // 16], U16, name="offsets")
+        scale_table = keep.tile([P, T], U8, name="scale_table", align_bytes=64)
+        word_table = keep.tile([P, T], I32, name="word_table", align_bytes=64)
+        raw = [keep.tile([P, PACK, N], F32, name="raw%d" % i, align_bytes=64) for i in range(3)]
+
+        nc.vector.memset(scale_table[:].bitcast(I32), 0)
+        nc.sync.dma_start(offsets[:], offs)
+        nc.sync.dma_start(raw[0][:], w1.rearrange("(p j) n -> p j n", j=PACK))
+        for q in range(4):
+            nc.sync.dma_start(
+                scale_table[32 * q : 32 * q + 4, :].bitcast(I32), x_scales[0, 4 * q : 4 * q + 4, :].bitcast(I32)
+            )
+        nc.sync.dma_start(word_table[:], x_words[0].rearrange("p n t -> p (n t)").bitcast(I32))
+        nc.sync.dma_start(raw[2][:], w3.rearrange("(p j) n -> p j n", j=PACK))
+        nc.sync.dma_start(raw[1][:], w2.rearrange("(p j) n -> p j n", j=PACK))
+
+        fm = keep.tile([P, HALVES, D], F32, name="fm")
+        ar = keep.tile([P, HALVES, D], F32, name="ar")
+        nc.sync.dma_start(fm[:], fmax[0].rearrange("(h p d) -> p h d", h=HALVES, d=D))
+        nc.sync.dma_start(ar[:], arm[0].rearrange("(h p d) -> p h d", h=HALVES, d=D))
+        ident = keep.tile([P, P], F32, name="ident", align_bytes=64)
+        make_identity(nc, ident[:])
+
+        def interleave(engine_copy, i):
+            grouped = keep.tile([P, N, PACK], BF16, name="grouped%d" % i, align_bytes=64)
+            engine_copy(
+                grouped[:].rearrange("p (c i) t -> p c t i", i=4),
+                raw[i][:].rearrange("p t (c i) -> p c t i", i=4),
+            )
+            return grouped
+
+        def quantize(grouped, i):
+            codes = keep.tile([P, N], U32, name="codes%d" % i, align_bytes=64)
+            scales = keep.tile([P, N], U8, name="scales%d" % i, align_bytes=64)
+            nc.vector.quantize_mx(
+                out=codes[:].bitcast(FP8X4), scales=scales[:], in_=grouped[:].rearrange("p n t -> p (n t)")
+            )
+            return codes, scales
+
+        def half_offsets(h):
+            return offsets[:, h * (HALF // 16) : (h + 1) * (HALF // 16)]
+
+        picked_scales = []
+        listed = []
+        for h in range(HALVES):
+            gathered = keep.tile([P, HALF], U8, name="listed_scales%d" % h, align_bytes=64)
+            nc.vector.tensor_copy(gathered[:], scale_table[:].indirect(half_offsets(h)))
+            listed.append(gathered)
+        for h in range(HALVES):
+            dealt = keep.tile([P, D, P], U8, name="picked_scales%d" % h, align_bytes=64)
+            nc.vector.tensor_copy(dealt[:], listed[h][:].rearrange("p (v d) -> p d v", d=D))
+            picked_scales.append(dealt)
+
+        quantized = {0: quantize(interleave(nc.scalar.copy, 0), 0)}
+
+        picked_words = []
+
+        def gather_words(h):
+            words = keep.tile([P, D, P], U32, name="picked_words%d" % h, align_bytes=64)
+            nc.vector.tensor_copy(
+                words[:].rearrange("p d v -> p v d"), word_table[:].bitcast(U32).indirect(half_offsets(h))
+            )
+            picked_words.append(words)
+
+        def product(h, pair, i):
+            bank = psum.tile([P, 2, N], F32, name="y%d_%d_%d" % (i, h, pair), tag="y%d_%d" % (i, pair))
+            codes, scales = quantized[i]
+            for e in range(2):
+                d = 2 * pair + e
+                nc.tensor.matmul_mx(
+                    out=bank[:, e, :],
+                    lhsT=picked_words[h][:, d, :].bitcast(FP8X4),
+                    lhsT_scale=picked_scales[h][:, d, :],
+                    rhs=codes[:].bitcast(FP8X4),
+                    rhs_scale=scales[:],
+                    start=True,
+                    stop=True,
+                )
+            return bank
+
+        def work_tile(name, h, pair):
+            return keep.tile([P, 2, N], F32, name="%s_%d_%d" % (name, h, pair), align_bytes=64)
+
+        def activate(name, h, pair, src, func, scale, bias=0.0):
+            dst = work_tile(name, h, pair)
+            nc.scalar.activation(dst[:], src[:], func, bias=bias, scale=scale)
+            return dst
+
+        def passive_part(h, pair, rise):
+            dst = work_tile("passive", h, pair)
+            for e in range(2):
+                d = 2 * pair + e
+                nc.vector.tensor_scalar(
+                    dst[:, e, :], rise[:, e, :], 1.0, g_passive[:, h, d : d + 1], ALU.max, ALU.mult
+                )
+            return dst
+
+        def weighted_bell(h, pair, bell):
+            dst = work_tile("weighted", h, pair)
+            for e in range(2):
+                d = 2 * pair + e
+                nc.vector.tensor_scalar(dst[:, e, :], bell[:, e, :], g_active[:, h, d : d + 1], None, ALU.mult)
+            return dst
+
+        def times_shifted(name, h, pair, t, shift, other):
+            dst = work_tile(name, h, pair)
+            nc.vector.scalar_tensor_tensor(dst[:], t[:], shift, other[:], ALU.add, ALU.mult)
+            return dst
+
+        def open_sums(h):
+            sums = [psum.tile([P, P], F32, name="sum%d_%d" % (h, m), tag="sum%d" % m) for m in range(2)]
+            for m in range(2):
+                nc.tensor.matmul(
+                    sums[m][:], g_rest[:, h : h + 1].to_broadcast([P, P]), ident[:],
+                    start=True, stop=False, is_transpose=True,
+                )
+            return sums
+
+        def add_turned(sums, part, last):
+            for e in range(2):
+                for m in range(2):
+                    nc.tensor.matmul(
+                        sums[m][:], part[:, e, m * P : (m + 1) * P], ident[:],
+                        start=False, stop=(last and e == 1), is_transpose=True,
+                    )
+
+        def store(h, sums):
+            result = keep.tile([P, 2, P], F32, name="result%d" % h, align_bytes=64)
+            nc.vector.tensor_copy(result[:, 0, :], sums[0][:])
+            nc.scalar.copy(result[:, 1, :], sums[1][:])
+            nc.sync.dma_start(out[:, h * P : (h + 1) * P].rearrange("(m p) v -> p m v", p=P), result[:])
+
+        half_log = 0.5 * math.log(19.0 / 7.0)
+
+        gather_words(0)
+        yl = [product(0, pair, 0) for pair in range(PAIRS)]
+        rise, bell = [], []
+        for pair in range(PAIRS):
+            rise.append(activate("rise", 0, pair, yl[pair], ACT.Exp, 0.9))
+            square = activate("square", 0, pair, yl[pair], ACT.Square, 1.0)
+            bell.append(activate("bell", 0, pair, square, ACT.Exp, -0.8))
+        gather_words(1)
+        grouped3 = interleave(nc.vector.tensor_copy, 2)
+        grouped2 = interleave(nc.vector.tensor_copy, 1)
+        quantized[2] = quantize(grouped3, 2)
+        quantized[1] = quantize(grouped2, 1)
+        g_active = keep.tile([P, HALVES, D], F32, name="g_active")
+        g_passive = keep.tile([P, HALVES, D], F32, name="g_passive")
+        g_minus = keep.tile([P, HALVES, D], F32, name="g_minus")
+        g_rest = keep.tile([P, HALVES], F32, name="g_rest")
+        nc.vector.scalar_tensor_tensor(g_active[:], fm[:], -5.0 / 7.0, ar[:], ALU.mult, ALU.mult)
+        nc.vector.scalar_tensor_tensor(g_passive[:], fm[:], 0.4, ar[:], ALU.mult, ALU.mult)
+        nc.vector.scalar_tensor_tensor(g_minus[:], fm[:], -0.4, ar[:], ALU.mult, ALU.mult)
+        nc.vector.tensor_reduce(g_rest[:], g_minus[:], mybir.AxisListType.X, ALU.add)
+        sums = open_sums(0)
+        weighted = [weighted_bell(0, pair, bell[pair]) for pair in range(PAIRS)]
+        for pair in range(PAIRS):
+            add_turned(sums, passive_part(0, pair, rise[pair]), False)
+        ya = [product(0, pair, 2) for pair in range(PAIRS)]
+        yv = [product(0, pair, 1) for pair in range(PAIRS)]
+        excited = []
+        for pair in range(PAIRS):
+            ta = activate("ta", 0, pair, ya[pair], ACT.Tanh, 0.5)
+            excited.append(times_shifted("excited", 0, pair, ta, 1.0, weighted[pair]))
+        for pair in range(PAIRS):
+            tv = activate("tv", 0, pair, yv[pair], ACT.Tanh, 1.0, half_log)
+            add_turned(sums, times_shifted("active", 0, pair, tv, -1.0, excited[pair]), pair == PAIRS - 1)
+        store(0, sums)
+
+        yl = [product(1, pair, 0) for pair in range(PAIRS)]
+        ya = [product(1, pair, 2) for pair in range(PAIRS)]
+        yv = [product(1, pair, 1) for pair in range(PAIRS)]
+        weighted = []
+        for pair in range(PAIRS):
+            square = activate("square", 1, pair, yl[pair], ACT.Square, 1.0)
+            weighted.append(weighted_bell(1, pair, activate("bell", 1, pair, square, ACT.Exp, -0.8)))
+        sums = open_sums(1)
+        excited = []
+        for pair in range(PAIRS):
+            ta = activate("ta", 1, pair, ya[pair], ACT.Tanh, 0.5)
+            excited.append(times_shifted("excited", 1, pair, ta, 1.0, weighted[pair]))
+        for pair in range(PAIRS):
+            tv = activate("tv", 1, pair, yv[pair], ACT.Tanh, 1.0, half_log)
+            add_turned(sums, times_shifted("active", 1, pair, tv, -1.0, excited[pair]), False)
+        for pair in range(PAIRS):
+            rise = activate("rise", 1, pair, yl[pair], ACT.Exp, 0.9)
+            add_turned(sums, passive_part(1, pair, rise), pair == PAIRS - 1)
+        store(1, sums)

@@ -36,11 +36,15 @@ def tile_picked_yhillm_mom_p_kernel(
         offsets = keep.tile([P, S // 16], U16, name="offsets")
         scale_table = keep.tile([P, T], U8, name="scale_table", align_bytes=64)
         word_table = keep.tile([P, T], I32, name="word_table", align_bytes=64)
-        raw = [keep.tile([P, PACK, N], F32, name="raw%d" % i, align_bytes=64) for i in range(3)]
+        raw = [keep.tile([P, PACK, N], F32, name="raw%d" % i, tag="raw%d" % i, align_bytes=64) for i in range(3)]
 
         nc.vector.memset(scale_table[:].bitcast(I32), 0)
         nc.sync.dma_start(offsets[:], offs)
         nc.sync.dma_start(raw[0][:], w1.rearrange("(p j) n -> p j n", j=PACK))
+        fm = keep.tile([P, HALVES, D], F32, name="fm")
+        ar = keep.tile([P, HALVES, D], F32, name="ar")
+        nc.sync.dma_start(fm[:], fmax[0].rearrange("(h p d) -> p h d", h=HALVES, d=D))
+        nc.sync.dma_start(ar[:], arm[0].rearrange("(h p d) -> p h d", h=HALVES, d=D))
         for q in range(4):
             nc.sync.dma_start(
                 scale_table[32 * q : 32 * q + 4, :].bitcast(I32), x_scales[0, 4 * q : 4 * q + 4, :].bitcast(I32)
@@ -49,19 +53,17 @@ def tile_picked_yhillm_mom_p_kernel(
         nc.sync.dma_start(raw[2][:], w3.rearrange("(p j) n -> p j n", j=PACK))
         nc.sync.dma_start(raw[1][:], w2.rearrange("(p j) n -> p j n", j=PACK))
 
-        fm = keep.tile([P, HALVES, D], F32, name="fm")
-        ar = keep.tile([P, HALVES, D], F32, name="ar")
-        nc.sync.dma_start(fm[:], fmax[0].rearrange("(h p d) -> p h d", h=HALVES, d=D))
-        nc.sync.dma_start(ar[:], arm[0].rearrange("(h p d) -> p h d", h=HALVES, d=D))
         ident = keep.tile([P, P], F32, name="ident", align_bytes=64)
         make_identity(nc, ident[:])
 
-        def interleave(engine_copy, i):
+        def interleave(i, scalar_columns):
             grouped = keep.tile([P, N, PACK], BF16, name="grouped%d" % i, align_bytes=64)
-            engine_copy(
-                grouped[:].rearrange("p (c i) t -> p c t i", i=4),
-                raw[i][:].rearrange("p t (c i) -> p c t i", i=4),
-            )
+            for copy, lo, hi in ((nc.scalar.copy, 0, scalar_columns), (nc.vector.tensor_copy, scalar_columns, N)):
+                if hi > lo:
+                    copy(
+                        grouped[:, lo:hi, :].rearrange("p (c i) t -> p c t i", i=4),
+                        raw[i][:, :, lo:hi].rearrange("p t (c i) -> p c t i", i=4),
+                    )
             return grouped
 
         def quantize(grouped, i):
@@ -86,7 +88,14 @@ def tile_picked_yhillm_mom_p_kernel(
             nc.vector.tensor_copy(dealt[:], listed[h][:].rearrange("p (v d) -> p d v", d=D))
             picked_scales.append(dealt)
 
-        quantized = {0: quantize(interleave(nc.scalar.copy, 0), 0)}
+        quantized = {0: quantize(interleave(0, N), 0)}
+
+        lever = keep.tile([P, HALVES, D], F32, name="lever")
+        lever_sum = keep.tile([P, HALVES], F32, name="lever_sum")
+        g_rest = keep.tile([P, HALVES], F32, name="g_rest")
+        nc.vector.tensor_tensor(lever[:], fm[:], ar[:], ALU.mult)
+        nc.vector.tensor_reduce(lever_sum[:], lever[:], mybir.AxisListType.X, ALU.add)
+        nc.vector.tensor_scalar(g_rest[:], lever_sum[:], -0.4, None, ALU.mult)
 
         picked_words = []
 
@@ -113,8 +122,13 @@ def tile_picked_yhillm_mom_p_kernel(
                 )
             return bank
 
+        held = ["square_0_0", "rise_0_0", "square_0_1", "rise_0_1"]
+
         def work_tile(name, h, pair):
-            return keep.tile([P, 2, N], F32, name="%s_%d_%d" % (name, h, pair), align_bytes=64)
+            full = "%s_%d_%d" % (name, h, pair)
+            if full in held:
+                return first[:, held.index(full)]
+            return keep.tile([P, 2, N], F32, name=full, align_bytes=64)[:]
 
         def activate(name, h, pair, src, func, scale, bias=0.0):
             dst = work_tile(name, h, pair)
@@ -126,7 +140,7 @@ def tile_picked_yhillm_mom_p_kernel(
             for e in range(2):
                 d = 2 * pair + e
                 nc.vector.tensor_scalar(
-                    dst[:, e, :], rise[:, e, :], 1.0, g_passive[:, h, d : d + 1], ALU.max, ALU.mult
+                    dst[:, e, :], rise[:, e, :], 0.4, lever[:, h, d : d + 1], ALU.max, ALU.mult
                 )
             return dst
 
@@ -134,7 +148,9 @@ def tile_picked_yhillm_mom_p_kernel(
             dst = work_tile("weighted", h, pair)
             for e in range(2):
                 d = 2 * pair + e
-                nc.vector.tensor_scalar(dst[:, e, :], bell[:, e, :], g_active[:, h, d : d + 1], None, ALU.mult)
+                nc.vector.tensor_scalar(
+                    dst[:, e, :], bell[:, e, :], lever[:, h, d : d + 1], -5.0 / 7.0, ALU.mult, ALU.mult
+                )
             return dst
 
         def times_shifted(name, h, pair, t, shift, other):
@@ -143,81 +159,89 @@ def tile_picked_yhillm_mom_p_kernel(
             return dst
 
         def open_sums(h):
-            sums = [psum.tile([P, P], F32, name="sum%d_%d" % (h, m), tag="sum%d" % m) for m in range(2)]
+            if h == 0:
+                both = psum.tile([P, 2, P], F32, name="sum0", tag="sum0")
+                sums = [both[:, m, :] for m in range(2)]
+            else:
+                both = None
+                low = psum.tile([P, P], F32, name="sum1_0", tag="sum1")
+                high = psum.tile([P, P], F32, name="sum1_1", tag="y0_0")
+                sums = [low[:], high[:]]
             for m in range(2):
                 nc.tensor.matmul(
-                    sums[m][:], g_rest[:, h : h + 1].to_broadcast([P, P]), ident[:],
-                    start=True, stop=False, is_transpose=True,
+                    sums[m], g_rest[:, h : h + 1].to_broadcast([P, P]), ident[:],
+                    start=(both is None or m == 0), stop=False, is_transpose=True,
                 )
-            return sums
+            return sums, both
 
-        def add_turned(sums, part, last):
+        def add_turned(opened, part, last):
+            sums, both = opened
             for e in range(2):
                 for m in range(2):
                     nc.tensor.matmul(
-                        sums[m][:], part[:, e, m * P : (m + 1) * P], ident[:],
-                        start=False, stop=(last and e == 1), is_transpose=True,
+                        sums[m], part[:, e, m * P : (m + 1) * P], ident[:],
+                        start=False, stop=(last and e == 1 and (both is None or m == 1)), is_transpose=True,
                     )
 
-        def store(h, sums):
+        def store(h, opened):
+            sums, both = opened
             result = keep.tile([P, 2, P], F32, name="result%d" % h, align_bytes=64)
-            nc.vector.tensor_copy(result[:, 0, :], sums[0][:])
-            nc.scalar.copy(result[:, 1, :], sums[1][:])
+            if both is None:
+                nc.vector.tensor_copy(result[:, 0, :], sums[0])
+                nc.scalar.copy(result[:, 1, :], sums[1])
+            else:
+                nc.vector.tensor_copy(result[:], both[:])
             nc.sync.dma_start(out[:, h * P : (h + 1) * P].rearrange("(m p) v -> p m v", p=P), result[:])
 
         half_log = 0.5 * math.log(19.0 / 7.0)
 
+        def length_stage(h, pair):
+            yl = product(h, pair, 0)
+            if (h, pair) == (1, 0):
+                plain, square = work_tile("plain", h, pair), work_tile("square", h, pair)
+                nc.vector.tensor_copy(plain, yl[:])
+                nc.vector.tensor_tensor(square, plain, plain, ALU.mult)
+                yl = plain
+            else:
+                square = activate("square", h, pair, yl, ACT.Square, 1.0)
+            rise = activate("rise", h, pair, yl, ACT.Exp, 0.9, math.log(0.4))
+            bell = activate("bell", h, pair, square, ACT.Exp, -0.8)
+            return rise, bell
+
+        def lever_stage(h, pair, sums, rise, bell):
+            add_turned(sums, passive_part(h, pair, rise), False)
+            return weighted_bell(h, pair, bell)
+
+        def force_stage(h, pair, sums, ya, yv, weighted):
+            ta, tv = work_tile("ta", h, pair), work_tile("tv", h, pair)
+            excited, active = work_tile("excited", h, pair), work_tile("active", h, pair)
+            last = h == HALVES - 1 and pair == PAIRS - 1
+            pieces = [slice(0, 1), slice(1, 2)] if last else [slice(0, 2)]
+            for s in pieces:
+                nc.scalar.activation(ta[:, s, :], ya[:, s, :], ACT.Tanh, scale=0.5)
+                nc.vector.scalar_tensor_tensor(excited[:, s, :], ta[:, s, :], 1.0, weighted[:, s, :], ALU.add, ALU.mult)
+            for s in pieces:
+                nc.scalar.activation(tv[:, s, :], yv[:, s, :], ACT.Tanh, bias=half_log, scale=1.0)
+                nc.vector.scalar_tensor_tensor(active[:, s, :], tv[:, s, :], -1.0, excited[:, s, :], ALU.add, ALU.mult)
+            add_turned(sums, active, pair == PAIRS - 1)
+
         gather_words(0)
-        yl = [product(0, pair, 0) for pair in range(PAIRS)]
-        rise, bell = [], []
-        for pair in range(PAIRS):
-            rise.append(activate("rise", 0, pair, yl[pair], ACT.Exp, 0.9))
-            square = activate("square", 0, pair, yl[pair], ACT.Square, 1.0)
-            bell.append(activate("bell", 0, pair, square, ACT.Exp, -0.8))
         gather_words(1)
-        grouped3 = interleave(nc.vector.tensor_copy, 2)
-        grouped2 = interleave(nc.vector.tensor_copy, 1)
-        quantized[2] = quantize(grouped3, 2)
-        quantized[1] = quantize(grouped2, 1)
-        g_active = keep.tile([P, HALVES, D], F32, name="g_active")
-        g_passive = keep.tile([P, HALVES, D], F32, name="g_passive")
-        g_minus = keep.tile([P, HALVES, D], F32, name="g_minus")
-        g_rest = keep.tile([P, HALVES], F32, name="g_rest")
-        nc.vector.scalar_tensor_tensor(g_active[:], fm[:], -5.0 / 7.0, ar[:], ALU.mult, ALU.mult)
-        nc.vector.scalar_tensor_tensor(g_passive[:], fm[:], 0.4, ar[:], ALU.mult, ALU.mult)
-        nc.vector.scalar_tensor_tensor(g_minus[:], fm[:], -0.4, ar[:], ALU.mult, ALU.mult)
-        nc.vector.tensor_reduce(g_rest[:], g_minus[:], mybir.AxisListType.X, ALU.add)
+        quantized[2] = quantize(interleave(2, N), 2)
+        first = keep.tile([P, 4, 2, N], F32, name="first", tag="raw2", align_bytes=64)
+        lengths = [length_stage(0, pair) for pair in range(PAIRS)]
+        quantized[1] = quantize(interleave(1, 0), 1)
+        banks = [(product(0, pair, 2), product(0, pair, 1)) for pair in range(PAIRS)]
         sums = open_sums(0)
-        weighted = [weighted_bell(0, pair, bell[pair]) for pair in range(PAIRS)]
+        weighted = [lever_stage(0, pair, sums, *lengths[pair]) for pair in range(PAIRS)]
         for pair in range(PAIRS):
-            add_turned(sums, passive_part(0, pair, rise[pair]), False)
-        ya = [product(0, pair, 2) for pair in range(PAIRS)]
-        yv = [product(0, pair, 1) for pair in range(PAIRS)]
-        excited = []
-        for pair in range(PAIRS):
-            ta = activate("ta", 0, pair, ya[pair], ACT.Tanh, 0.5)
-            excited.append(times_shifted("excited", 0, pair, ta, 1.0, weighted[pair]))
-        for pair in range(PAIRS):
-            tv = activate("tv", 0, pair, yv[pair], ACT.Tanh, 1.0, half_log)
-            add_turned(sums, times_shifted("active", 0, pair, tv, -1.0, excited[pair]), pair == PAIRS - 1)
+            force_stage(0, pair, sums, *banks[pair], weighted[pair])
         store(0, sums)
 
-        yl = [product(1, pair, 0) for pair in range(PAIRS)]
-        ya = [product(1, pair, 2) for pair in range(PAIRS)]
-        yv = [product(1, pair, 1) for pair in range(PAIRS)]
-        weighted = []
         for pair in range(PAIRS):
-            square = activate("square", 1, pair, yl[pair], ACT.Square, 1.0)
-            weighted.append(weighted_bell(1, pair, activate("bell", 1, pair, square, ACT.Exp, -0.8)))
-        sums = open_sums(1)
-        excited = []
-        for pair in range(PAIRS):
-            ta = activate("ta", 1, pair, ya[pair], ACT.Tanh, 0.5)
-            excited.append(times_shifted("excited", 1, pair, ta, 1.0, weighted[pair]))
-        for pair in range(PAIRS):
-            tv = activate("tv", 1, pair, yv[pair], ACT.Tanh, 1.0, half_log)
-            add_turned(sums, times_shifted("active", 1, pair, tv, -1.0, excited[pair]), False)
-        for pair in range(PAIRS):
-            rise = activate("rise", 1, pair, yl[pair], ACT.Exp, 0.9)
-            add_turned(sums, passive_part(1, pair, rise), pair == PAIRS - 1)
+            length = length_stage(1, pair)
+            if pair == 0:
+                sums = open_sums(1)
+            ya, yv = product(1, pair, 2), product(1, pair, 1)
+            force_stage(1, pair, sums, ya, yv, lever_stage(1, pair, sums, *length))
         store(1, sums)

import math
from contextlib import ExitStack

import concourse.mybir as mybir
from concourse.masks import make_identity

K, T, S, D, N = 512, 4096, 1024, 4, 256
FLOPS = 3 * 2 * K * N * S
BYTES = K * T + (K // 32) * T + 3 * K * N * 4 + 2 * S * 4 + 128 * (S // 16) * 2 + N * (S // D) * 4

F32 = mybir.dt.float32
BF16 = mybir.dt.bfloat16
I32 = mybir.dt.int32
U32 = mybir.dt.uint32
U16 = mybir.dt.uint16
U8 = mybir.dt.uint8
FP8X4 = mybir.dt.float8_e4m3fn_x4
ALU = mybir.AluOpType
ACT = mybir.ActivationFunctionType

P = 128
PACK = 4
HALVES = 2
HALF = S // HALVES
PAIRS = 2


def tile_picked_yhillm_mom_p_kernel(
    tc, x_words, x_scales, w1, w2, w3, fmax, arm, offs, out
):
    nc = tc.nc
    with ExitStack() as ctx:
        keep = ctx.enter_context(tc.tile_pool(name="keep", bufs=1))
        psum = ctx.enter_context(tc.psum_pool(name="psum", bufs=1))

        offsets = keep.tile([P, S // 16], U16, name="offsets")
        scale_table = keep.tile([P, T], U8, name="scale_table", align_bytes=64)
        word_table = keep.tile([P, T], I32, name="word_table", align_bytes=64)
        raw = [keep.tile([P, PACK, N], F32, name="raw%d" % i, tag="raw%d" % i, align_bytes=64) for i in range(3)]

        nc.vector.memset(scale_table[:].bitcast(I32), 0)
        nc.sync.dma_start(offsets[:], offs)
        nc.sync.dma_start(raw[0][:], w1.rearrange("(p j) n -> p j n", j=PACK))
        fm = keep.tile([P, HALVES, D], F32, name="fm")
        ar = keep.tile([P, HALVES, D], F32, name="ar")
        nc.sync.dma_start(fm[:], fmax[0].rearrange("(h p d) -> p h d", h=HALVES, d=D))
        nc.sync.dma_start(ar[:], arm[0].rearrange("(h p d) -> p h d", h=HALVES, d=D))
        for q in range(4):
            nc.sync.dma_start(
                scale_table[32 * q : 32 * q + 4, :].bitcast(I32), x_scales[0, 4 * q : 4 * q + 4, :].bitcast(I32)
            )
        nc.sync.dma_start(word_table[:], x_words[0].rearrange("p n t -> p (n t)").bitcast(I32))
        nc.sync.dma_start(raw[2][:], w3.rearrange("(p j) n -> p j n", j=PACK))
        nc.sync.dma_start(raw[1][:], w2.rearrange("(p j) n -> p j n", j=PACK))

        ident = keep.tile([P, P], F32, name="ident", align_bytes=64)
        make_identity(nc, ident[:])

        def interleave(i, scalar_columns):
            grouped = keep.tile([P, N, PACK], BF16, name="grouped%d" % i, align_bytes=64)
            for copy, lo, hi in ((nc.scalar.copy, 0, scalar_columns), (nc.vector.tensor_copy, scalar_columns, N)):
                if hi > lo:
                    copy(
                        grouped[:, lo:hi, :].rearrange("p (c i) t -> p c t i", i=4),
                        raw[i][:, :, lo:hi].rearrange("p t (c i) -> p c t i", i=4),
                    )
            return grouped

        def quantize(grouped, i):
            codes = keep.tile([P, N], U32, name="codes%d" % i, align_bytes=64)
            scales = keep.tile([P, N], U8, name="scales%d" % i, align_bytes=64)
            nc.vector.quantize_mx(
                out=codes[:].bitcast(FP8X4), scales=scales[:], in_=grouped[:].rearrange("p n t -> p (n t)")
            )
            return codes, scales

        def half_offsets(h):
            return offsets[:, h * (HALF // 16) : (h + 1) * (HALF // 16)]

        picked_scales = []
        listed = []
        for h in range(HALVES):
            gathered = keep.tile([P, HALF], U8, name="listed_scales%d" % h, align_bytes=64)
            nc.vector.tensor_copy(gathered[:], scale_table[:].indirect(half_offsets(h)))
            listed.append(gathered)
        for h in range(HALVES):
            dealt = keep.tile([P, D, P], U8, name="picked_scales%d" % h, align_bytes=64)
            nc.vector.tensor_copy(dealt[:], listed[h][:].rearrange("p (v d) -> p d v", d=D))
            picked_scales.append(dealt)

        quantized = {0: quantize(interleave(0, N), 0)}

        lever = keep.tile([P, HALVES, D], F32, name="lever")
        lever_sum = keep.tile([P, HALVES], F32, name="lever_sum")
        g_rest = keep.tile([P, HALVES], F32, name="g_rest")
        nc.vector.tensor_tensor(lever[:], fm[:], ar[:], ALU.mult)
        nc.vector.tensor_reduce(lever_sum[:], lever[:], mybir.AxisListType.X, ALU.add)
        nc.vector.tensor_scalar(g_rest[:], lever_sum[:], -0.4, None, ALU.mult)

        picked_words = []

        def gather_words(h):
            words = keep.tile([P, D, P], U32, name="picked_words%d" % h, align_bytes=64)
            nc.vector.tensor_copy(
                words[:].rearrange("p d v -> p v d"), word_table[:].bitcast(U32).indirect(half_offsets(h))
            )
            picked_words.append(words)

        def product(h, pair, i):
            bank = psum.tile([P, 2, N], F32, name="y%d_%d_%d" % (i, h, pair), tag="y%d_%d" % (i, pair))
            codes, scales = quantized[i]
            for e in range(2):
                d = 2 * pair + e
                nc.tensor.matmul_mx(
                    out=bank[:, e, :],
                    lhsT=picked_words[h][:, d, :].bitcast(FP8X4),
                    lhsT_scale=picked_scales[h][:, d, :],
                    rhs=codes[:].bitcast(FP8X4),
                    rhs_scale=scales[:],
                    start=True,
                    stop=True,
                )
            return bank

        held = ["square_0_0", "rise_0_0", "square_0_1", "rise_0_1"]

        def work_tile(name, h, pair):
            full = "%s_%d_%d" % (name, h, pair)
            if full in held:
                return first[:, held.index(full)]
            return keep.tile([P, 2, N], F32, name=full, align_bytes=64)[:]

        def activate(name, h, pair, src, func, scale, bias=0.0):
            dst = work_tile(name, h, pair)
            nc.scalar.activation(dst[:], src[:], func, bias=bias, scale=scale)
            return dst

        def passive_part(h, pair, rise):
            dst = work_tile("passive", h, pair)
            for e in range(2):
                d = 2 * pair + e
                nc.vector.tensor_scalar(
                    dst[:, e, :], rise[:, e, :], 0.4, lever[:, h, d : d + 1], ALU.max, ALU.mult
                )
            return dst

        def weighted_bell(h, pair, bell):
            dst = work_tile("weighted", h, pair)
            for e in range(2):
                d = 2 * pair + e
                nc.vector.tensor_scalar(
                    dst[:, e, :], bell[:, e, :], lever[:, h, d : d + 1], -5.0 / 7.0, ALU.mult, ALU.mult
                )
            return dst

        def times_shifted(name, h, pair, t, shift, other):
            dst = work_tile(name, h, pair)
            nc.vector.scalar_tensor_tensor(dst[:], t[:], shift, other[:], ALU.add, ALU.mult)
            return dst

        def open_sums(h):
            if h == 0:
                both = psum.tile([P, 2, P], F32, name="sum0", tag="sum0")
                sums = [both[:, m, :] for m in range(2)]
            else:
                both = None
                low = psum.tile([P, P], F32, name="sum1_0", tag="sum1")
                high = psum.tile([P, P], F32, name="sum1_1", tag="y0_0")
                sums = [low[:], high[:]]
            for m in range(2):
                nc.tensor.matmul(
                    sums[m], g_rest[:, h : h + 1].to_broadcast([P, P]), ident[:],
                    start=(both is None or m == 0), stop=False, is_transpose=True,
                )
            return sums, both

        def add_turned(opened, part, last):
            sums, both = opened
            for e in range(2):
                for m in range(2):
                    nc.tensor.matmul(
                        sums[m], part[:, e, m * P : (m + 1) * P], ident[:],
                        start=False, stop=(last and e == 1 and (both is None or m == 1)), is_transpose=True,
                    )

        def store(h, opened):
            sums, both = opened
            result = keep.tile([P, 2, P], F32, name="result%d" % h, align_bytes=64)
            if both is None:
                nc.vector.tensor_copy(result[:, 0, :], sums[0])
                nc.scalar.copy(result[:, 1, :], sums[1])
            else:
                nc.vector.tensor_copy(result[:], both[:])
            nc.sync.dma_start(out[:, h * P : (h + 1) * P].rearrange("(m p) v -> p m v", p=P), result[:])

        half_log = 0.5 * math.log(19.0 / 7.0)

        def length_stage(h, pair):
            yl = product(h, pair, 0)
            if (h, pair) == (1, 0):
                plain, square = work_tile("plain", h, pair), work_tile("square", h, pair)
                nc.vector.tensor_copy(plain, yl[:])
                nc.vector.tensor_tensor(square, plain, plain, ALU.mult)
                yl = plain
            else:
                square = activate("square", h, pair, yl, ACT.Square, 1.0)
            rise = activate("rise", h, pair, yl, ACT.Exp, 0.9, math.log(0.4))
            bell = activate("bell", h, pair, square, ACT.Exp, -0.8)
            return rise, bell

        def lever_stage(h, pair, sums, rise, bell):
            add_turned(sums, passive_part(h, pair, rise), False)
            return weighted_bell(h, pair, bell)

        def force_stage(h, pair, sums, ya, yv, weighted):
            ta, tv = work_tile("ta", h, pair), work_tile("tv", h, pair)
            excited, active = work_tile("excited", h, pair), work_tile("active", h, pair)
            last = h == HALVES - 1 and pair == PAIRS - 1
            pieces = [slice(0, 1), slice(1, 2)] if last else [slice(0, 2)]
            for s in pieces:
                nc.scalar.activation(ta[:, s, :], ya[:, s, :], ACT.Tanh, scale=0.5)
                nc.vector.scalar_tensor_tensor(excited[:, s, :], ta[:, s, :], 1.0, weighted[:, s, :], ALU.add, ALU.mult)
            for s in pieces:
                nc.scalar.activation(tv[:, s, :], yv[:, s, :], ACT.Tanh, bias=half_log, scale=1.0)
                nc.vector.scalar_tensor_tensor(active[:, s, :], tv[:, s, :], -1.0, excited[:, s, :], ALU.add, ALU.mult)
            add_turned(sums, active, pair == PAIRS - 1)

        gather_words(0)
        gather_words(1)
        quantized[2] = quantize(interleave(2, N), 2)
        first = keep.tile([P, 4, 2, N], F32, name="first", tag="raw2", align_bytes=64)
        lengths = [length_stage(0, pair) for pair in range(PAIRS)]
        quantized[1] = quantize(interleave(1, 0), 1)
        banks = [(product(0, pair, 2), product(0, pair, 1)) for pair in range(PAIRS)]
        sums = open_sums(0)
        weighted = [lever_stage(0, pair, sums, *lengths[pair]) for pair in range(PAIRS)]
        for pair in range(PAIRS):
            force_stage(0, pair, sums, *banks[pair], weighted[pair])
        store(0, sums)

        for pair in range(PAIRS):
            length = length_stage(1, pair)
            if pair == 0:
                sums = open_sums(1)
            ya, yv = product(1, pair, 2), product(1, pair, 1)
            force_stage(1, pair, sums, ya, yv, lever_stage(1, pair, sums, *length))
        store(1, sums)
